import numpy as np
import ml_dtypes


def mxq(x, axis, fmt="e4m3"):
    dtype, down = {"e4m3": (ml_dtypes.float8_e4m3fn, 7), "e5m2": (ml_dtypes.float8_e5m2, 14)}[fmt]
    v = np.moveaxis(np.asarray(x, np.float32).astype(ml_dtypes.bfloat16).astype(np.float64), axis, -1)
    blocks = v.reshape(v.shape[:-1] + (-1, 32))
    amax = np.abs(blocks).max(-1, keepdims=True)
    byte = np.maximum(np.where(amax > 0, np.frexp(amax)[1] - 1 + 127, 0) - down, 1)
    scale = np.exp2(byte - 127.0)
    codes = (blocks / scale).astype(np.float32).astype(dtype).astype(np.float64)
    return np.moveaxis((codes * scale).reshape(v.shape), -1, axis)


WIDE = False


def mx_kscale(k, group=512):
    if not WIDE:
        return np.ones(k)
    levels = np.array([18, -18])
    if group != 512:
        return np.exp2(np.random.permutation(np.resize(levels, k // group))).repeat(group)
    if k % 512:
        return np.exp2(np.random.permutation(np.resize(levels, k // 32))).repeat(32)
    a = np.empty((k // 512, 16))
    for p in range(k // 512):
        a[p, :8] = np.random.permutation(np.resize(levels, 8))
        for g in range(8):
            far = levels[np.abs(levels - a[p, g]) >= 10]
            a[p, g + 8] = far[np.random.randint(len(far))]
    return np.exp2(a.ravel()).repeat(32)


def f64(x):
    return np.asarray(x).astype(np.float64)


K, R, M, N = 1024, 128, 512, 512


def setup_inputs():
    n = np.random.standard_normal
    s = mx_kscale(K)[:, None]
    z = mx_kscale(R, 0)
    return {
        "x": (n((K, N)) * s).astype(np.float32),
        "w": (n((K, M)) / np.sqrt(K) / s).astype(np.float32),
        "a": (n((K, R)) / np.sqrt(K) / s * z).astype(np.float32),
        "bb": (n((R, M)) / np.sqrt(R) / z[:, None]).astype(np.float32),
    }


def reference(x, w, a, bb):
    xq = mxq(f64(x), 0, "e4m3")
    z = mxq(f64(a), 0, "e4m3").T @ xq
    y = (mxq(f64(w), 0, "e4m3").T @ xq) + (mxq(f64(bb), 0, "e4m3").T @ mxq(z, 0, "e4m3"))
    y = np.square(np.maximum(y, 0.0))
    return y

@@ -1,0 +1,225 @@
+from contextlib import ExitStack
+
+import concourse.mybir as mybir
+
+K, R, M, N = 1024, 128, 512, 512
+FLOPS = 2 * N * (K * M + K * R + R * M)
+
+F32 = mybir.dt.float32
+BF16 = mybir.dt.bfloat16
+I32 = mybir.dt.int32
+U8 = mybir.dt.uint8
+FP8X4 = mybir.dt.float8_e4m3fn_x4
+ALU = mybir.AluOpType
+
+P = 128
+PACK = 4
+K_PASS = P * PACK
+PASSES = K // K_PASS
+BLK = 128
+BLOCKS = 4
+ROWS = 32
+HALF = 2 * BLK
+
+
+def tile_rows_lora_relu2_kernel(tc, x, w, a, bb, out):
+    nc = tc.nc
+    with ExitStack() as ctx:
+        sb = ctx.enter_context(tc.tile_pool(name="sb", bufs=1))
+        ps = ctx.enter_context(tc.psum_pool(name="ps", bufs=1))
+        ctx.enter_context(tc.manual_schedule())
+
+        whole = [ps.tile([P, 512], F32, name="whole%d" % i) for i in range(BLOCKS)]
+        rowbank = [ps.tile([P, 512], F32, name="row%d" % i) for i in range(BLOCKS)]
+
+        def operand(name, words):
+            grouped = sb.tile([P, words * PACK], BF16, name=name + "_g", align_bytes=64)
+            codes = sb.tile([P, words], I32, name=name + "_c", align_bytes=64)
+            scales = sb.tile([P, words], U8, name=name + "_s", align_bytes=64)
+            return grouped, codes, scales
+
+        def load_half(src, name, c, h):
+            raw = sb.tile([P, PACK, HALF], F32, name="%s_raw%d%d" % (name, c, h))
+            rows = src[c * K_PASS : (c + 1) * K_PASS, h * HALF : (h + 1) * HALF]
+            nc.sync.dma_start(out=raw[:], in_=rows.rearrange("(p j) n -> p j n", j=PACK))
+            return raw
+
+        def interleave(eng, grouped, raw_cols):
+            dst = grouped.rearrange("p (c i t) -> p c t i", i=4, t=PACK)
+            src = raw_cols.rearrange("p t (c i) -> p c t i", i=4)
+            if eng == "v":
+                nc.vector.tensor_copy(out=dst, in_=src)
+            else:
+                nc.scalar.copy(out=dst, in_=src)
+
+        def quantize(op):
+            grouped, codes, scales = op
+            nc.vector.quantize_mx(out=codes[:].bitcast(FP8X4), scales=scales[:], in_=grouped[:])
+
+        a_raw = sb.tile([P, PASSES, PACK * R], F32, name="a_raw")
+        nc.sync.dma_start(out=a_raw[:], in_=a.rearrange("(c p j) r -> p c (j r)", c=PASSES, j=PACK))
+        x_raw = {}
+        for h in range(2):
+            for c in range(PASSES):
+                x_raw[c, h] = load_half(x, "x", c, h)
+        bb_raw = sb.tile([P, PACK, BLK], F32, name="bb_raw")
+        for g in range(BLOCKS):
+            nc.sync.dma_start(
+                out=bb_raw[g * ROWS : (g + 1) * ROWS],
+                in_=bb[:, g * BLK : (g + 1) * BLK].rearrange("(p j) m -> p j m", j=PACK),
+            )
+        w_raw = {}
+        for h in range(2):
+            for c in range(PASSES):
+                w_raw[c, h] = load_half(w, "w", c, h)
+
+        xq = {(c, b): operand("x%d%d" % (c, b), BLK) for c in range(PASSES) for b in range(BLOCKS)}
+        wq = {(c, b): operand("w%d%d" % (c, b), BLK) for c in range(PASSES) for b in range(BLOCKS)}
+        zq = [operand("z%d" % b, BLK) for b in range(BLOCKS)]
+        bq = operand("bb", BLK)
+        aq = operand("a", PASSES * R)
+        a_codes = sb.tile([P, PASSES * PACK, BLOCKS, ROWS], I32, name="a_rep_c", align_bytes=64)
+        a_scales = sb.tile([P, PASSES * PACK * BLK], U8, name="a_rep_s", align_bytes=64)
+        lora = [sb.tile([P, N], F32, name="lora%d" % b) for b in range(BLOCKS)]
+        ysum = [sb.tile([P, N], F32, name="y%d" % b) for b in range(BLOCKS)]
+        res = [sb.tile([P, N], F32, name="res%d" % b) for b in range(BLOCKS)]
+
+        def prep_a():
+            grouped, codes, scales = aq
+            nc.vector.memset(scales[:].bitcast(I32), 0)
+            for c, copy in ((0, nc.vector.tensor_copy), (1, nc.scalar.copy)):
+                copy(
+                    out=grouped[:, c * 512 : (c + 1) * 512].rearrange("p (s q j) -> p s q j", s=PACK, j=PACK),
+                    in_=a_raw[:, c, :].rearrange("p (j q s) -> p s q j", j=PACK, s=PACK),
+                )
+            quantize(aq)
+
+        def repeat_a():
+            grouped, codes, scales = aq
+            nc.vector.tensor_copy(
+                out=a_codes[:],
+                in_=codes[:].rearrange("p (e q) -> p e q", q=ROWS).unsqueeze(2).to_broadcast([P, 8, BLOCKS, ROWS]),
+            )
+            nc.vector.tensor_copy(
+                out=a_scales[:].bitcast(I32).rearrange("p (e g q) -> p e g q", e=8, g=BLOCKS),
+                in_=scales[:].bitcast(I32).rearrange("p (e q) -> p e q", e=8).unsqueeze(2).to_broadcast([P, 8, BLOCKS, 8]),
+            )
+
+        def copy_blk(eng, ops, raws, c, b):
+            raw = raws[c, b // 2]
+            interleave(eng, ops[c, b][0][:], raw[:, :, (b % 2) * BLK : (b % 2 + 1) * BLK])
+
+        def z_mm(b):
+            for s in range(PACK):
+                for c in range(PASSES):
+                    e = c * PACK + s
+                    nc.tensor.matmul_mx(
+                        out=whole[b][:, s * BLK : (s + 1) * BLK],
+                        lhsT=a_codes[:, e].rearrange("p g q -> p (g q)").bitcast(FP8X4),
+                        lhsT_scale=a_scales[:, e * BLK : (e + 1) * BLK],
+                        rhs=xq[c, b][1][:].bitcast(FP8X4),
+                        rhs_scale=xq[c, b][2][:],
+                        start=(c == 0),
+                        stop=(c == PASSES - 1),
+                    )
+
+        def z_out(b):
+            nc.scalar.copy(
+                out=zq[b][0][:].rearrange("p (n s) -> p n s", s=PACK),
+                in_=whole[b][:].rearrange("p (s n) -> p n s", s=PACK),
+            )
+
+        def lora_mm(b):
+            for g in range(BLOCKS):
+                rows = slice(g * ROWS, (g + 1) * ROWS)
+                nc.tensor.matmul_mx(
+                    out=rowbank[g][:, b * BLK : (b + 1) * BLK],
+                    lhsT=bq[1][rows, :].bitcast(FP8X4),
+                    lhsT_scale=bq[2][rows, :],
+                    rhs=zq[b][1][rows, :].bitcast(FP8X4),
+                    rhs_scale=zq[b][2][rows, :],
+                    start=True,
+                    stop=True,
+                )
+
+        def lora_out(m):
+            nc.scalar.copy(out=lora[m][:], in_=rowbank[m][:])
+
+        def main_mm(m):
+            for b in range(BLOCKS):
+                for c in range(PASSES):
+                    nc.tensor.matmul_mx(
+                        out=whole[m][:, b * BLK : (b + 1) * BLK],
+                        lhsT=wq[c, m][1][:].bitcast(FP8X4),
+                        lhsT_scale=wq[c, m][2][:],
+                        rhs=xq[c, b][1][:].bitcast(FP8X4),
+                        rhs_scale=xq[c, b][2][:],
+                        start=(c == 0),
+                        stop=(c == PASSES - 1),
+                    )
+
+        def add(m):
+            nc.vector.tensor_tensor(out=ysum[m][:], in0=whole[m][:], in1=lora[m][:], op=ALU.add)
+
+        def relu2(m):
+            nc.vector.scalar_tensor_tensor(
+                out=res[m][:], in0=ysum[m][:], scalar=0.0, in1=ysum[m][:], op0=ALU.max, op1=ALU.mult
+            )
+            nc.sync.dma_start(out=out[m * BLK : (m + 1) * BLK, :], in_=res[m][:])
+
+        def piece(ops, raws, c, h):
+            copy_blk("s", ops, raws, c, 2 * h)
+            copy_blk("v", ops, raws, c, 2 * h + 1)
+            quantize(ops[c, 2 * h])
+            quantize(ops[c, 2 * h + 1])
+
+        prep_a()
+        copy_blk("s", xq, x_raw, 0, 0)
+        copy_blk("v", xq, x_raw, 0, 1)
+        repeat_a()
+        quantize(xq[0, 0])
+        quantize(xq[0, 1])
+        piece(xq, x_raw, 1, 0)
+        z_mm(0)
+        z_mm(1)
+        piece(xq, x_raw, 0, 1)
+        z_out(0)
+        piece(xq, x_raw, 1, 1)
+        z_out(1)
+        z_mm(2)
+        z_mm(3)
+        interleave("v", bq[0][:], bb_raw[:])
+        quantize(zq[0])
+        quantize(bq)
+        quantize(zq[1])
+        z_out(2)
+        z_out(3)
+        lora_mm(0)
+        lora_mm(1)
+        copy_blk("v", wq, w_raw, 0, 0)
+        copy_blk("v", wq, w_raw, 0, 1)
+        quantize(zq[2])
+        quantize(wq[0, 0])
+        quantize(zq[3])
+        quantize(wq[0, 1])
+        lora_mm(2)
+        lora_mm(3)
+        piece(wq, w_raw, 1, 0)
+        main_mm(0)
+        main_mm(1)
+        lora_out(0)
+        lora_out(1)
+        piece(wq, w_raw, 0, 1)
+        add(0)
+        add(1)
+        lora_out(2)
+        relu2(0)
+        piece(wq, w_raw, 1, 1)
+        main_mm(2)
+        main_mm(3)
+        lora_out(3)
+        relu2(1)
+        add(2)
+        add(3)
+        relu2(2)
+        relu2(3)

@@ -11,215 +11,241 @@ I32 = mybir.dt.int32
 U8 = mybir.dt.uint8
 FP8X4 = mybir.dt.float8_e4m3fn_x4
 ALU = mybir.AluOpType
+ACT = mybir.ActivationFunctionType
 
 P = 128
 PACK = 4
 K_PASS = P * PACK
 PASSES = K // K_PASS
 BLK = 128
-BLOCKS = 4
-ROWS = 32
-HALF = 2 * BLK
+BLOCKS = N // BLK
+ROWS = R // PACK
+PAIR = 2
+ALL = slice(0, N)
+LEFT, RIGHT = slice(0, N // 2), slice(N // 2, N)
+WARM_BEFORE_Z = 14
+WARM_BEFORE_LAST_LORA = 8
+
+assert M == N and BLOCKS * ROWS == P
 
 
 def tile_rows_lora_relu2_kernel(tc, x, w, a, bb, out):
     nc = tc.nc
+    on_vector, on_scalar = nc.vector.tensor_copy, nc.scalar.copy
     with ExitStack() as ctx:
         sb = ctx.enter_context(tc.tile_pool(name="sb", bufs=1))
         ps = ctx.enter_context(tc.psum_pool(name="ps", bufs=1))
         ctx.enter_context(tc.manual_schedule())
 
-        whole = [ps.tile([P, 512], F32, name="whole%d" % i) for i in range(BLOCKS)]
-        rowbank = [ps.tile([P, 512], F32, name="row%d" % i) for i in range(BLOCKS)]
+        whole_bank = [ps.tile([P, N], F32, name="whole%d" % i) for i in range(BLOCKS)]
+        row_bank = [ps.tile([P, N], F32, name="row%d" % g) for g in range(BLOCKS)]
 
-        def operand(name, words):
-            grouped = sb.tile([P, words * PACK], BF16, name=name + "_g", align_bytes=64)
-            codes = sb.tile([P, words], I32, name=name + "_c", align_bytes=64)
-            scales = sb.tile([P, words], U8, name=name + "_s", align_bytes=64)
+        def mx_operand(name, columns):
+            grouped = sb.tile([P, columns * PACK], BF16, name=name + "_grouped", align_bytes=64)
+            codes = sb.tile([P, columns], I32, name=name + "_codes", align_bytes=64)
+            scales = sb.tile([P, columns], U8, name=name + "_scales", align_bytes=64)
             return grouped, codes, scales
 
-        def load_half(src, name, c, h):
-            raw = sb.tile([P, PACK, HALF], F32, name="%s_raw%d%d" % (name, c, h))
-            rows = src[c * K_PASS : (c + 1) * K_PASS, h * HALF : (h + 1) * HALF]
+        def load(src, name, c, first, count):
+            raw = sb.tile([P, PACK, count * BLK], F32, name="%s_raw%d%d" % (name, c, first))
+            rows = src[c * K_PASS : (c + 1) * K_PASS, first * BLK : (first + count) * BLK]
             nc.sync.dma_start(out=raw[:], in_=rows.rearrange("(p j) n -> p j n", j=PACK))
-            return raw
-
-        def interleave(eng, grouped, raw_cols):
-            dst = grouped.rearrange("p (c i t) -> p c t i", i=4, t=PACK)
-            src = raw_cols.rearrange("p t (c i) -> p c t i", i=4)
-            if eng == "v":
-                nc.vector.tensor_copy(out=dst, in_=src)
-            else:
-                nc.scalar.copy(out=dst, in_=src)
-
-        def quantize(op):
-            grouped, codes, scales = op
-            nc.vector.quantize_mx(out=codes[:].bitcast(FP8X4), scales=scales[:], in_=grouped[:])
+            return {(c, first + i): raw[:, :, i * BLK : (i + 1) * BLK] for i in range(count)}
 
         a_raw = sb.tile([P, PASSES, PACK * R], F32, name="a_raw")
         nc.sync.dma_start(out=a_raw[:], in_=a.rearrange("(c p j) r -> p c (j r)", c=PASSES, j=PACK))
-        x_raw = {}
-        for h in range(2):
-            for c in range(PASSES):
-                x_raw[c, h] = load_half(x, "x", c, h)
+        x_raw = {**load(x, "x", 0, 0, 4), **load(x, "x", 1, 0, 2), **load(x, "x", 1, 2, 2)}
         bb_raw = sb.tile([P, PACK, BLK], F32, name="bb_raw")
         for g in range(BLOCKS):
             nc.sync.dma_start(
                 out=bb_raw[g * ROWS : (g + 1) * ROWS],
                 in_=bb[:, g * BLK : (g + 1) * BLK].rearrange("(p j) m -> p j m", j=PACK),
             )
-        w_raw = {}
-        for h in range(2):
-            for c in range(PASSES):
-                w_raw[c, h] = load_half(w, "w", c, h)
+        w_raw = {**load(w, "w", 0, 0, 2), **load(w, "w", 1, 0, 2)}
+        w_raw = {**w_raw, **load(w, "w", 0, 2, 2), **load(w, "w", 1, 2, 1), **load(w, "w", 1, 3, 1)}
 
-        xq = {(c, b): operand("x%d%d" % (c, b), BLK) for c in range(PASSES) for b in range(BLOCKS)}
-        wq = {(c, b): operand("w%d%d" % (c, b), BLK) for c in range(PASSES) for b in range(BLOCKS)}
-        zq = [operand("z%d" % b, BLK) for b in range(BLOCKS)]
-        bq = operand("bb", BLK)
-        aq = operand("a", PASSES * R)
-        a_codes = sb.tile([P, PASSES * PACK, BLOCKS, ROWS], I32, name="a_rep_c", align_bytes=64)
-        a_scales = sb.tile([P, PASSES * PACK * BLK], U8, name="a_rep_s", align_bytes=64)
-        lora = [sb.tile([P, N], F32, name="lora%d" % b) for b in range(BLOCKS)]
-        ysum = [sb.tile([P, N], F32, name="y%d" % b) for b in range(BLOCKS)]
-        res = [sb.tile([P, N], F32, name="res%d" % b) for b in range(BLOCKS)]
+        x_mx = {key: mx_operand("x%d%d" % key, BLK) for key in sorted(x_raw)}
+        w_mx = {key: mx_operand("w%d%d" % key, BLK) for key in sorted(w_raw)}
+        z_mx = [mx_operand("z%d" % b, BLK) for b in range(BLOCKS)]
+        bb_mx = mx_operand("bb", BLK)
+        a_grouped, a_codes, a_scales = a_mx = mx_operand("a", PASSES * R)
+        a_operands = PASSES * PACK
+        a_codes_x4 = sb.tile([P, a_operands, BLOCKS, ROWS], I32, name="a_codes_x4", align_bytes=64)
+        a_scales_x4 = sb.tile([P, a_operands * BLK], U8, name="a_scales_x4", align_bytes=64)
+        lora = [sb.tile([P, N], F32, name="lora%d" % m) for m in range(BLOCKS)]
+        y = [sb.tile([P, N], F32, name="y%d" % m) for m in range(BLOCKS)]
+        result = [sb.tile([P, N], F32, name="result%d" % m) for m in range(BLOCKS)]
+        relu_left = {m: sb.tile([P, N // 2], F32, name="relu%d" % m) for m in range(1, BLOCKS)}
 
-        def prep_a():
-            grouped, codes, scales = aq
-            nc.vector.memset(scales[:].bitcast(I32), 0)
-            for c, copy in ((0, nc.vector.tensor_copy), (1, nc.scalar.copy)):
-                copy(
-                    out=grouped[:, c * 512 : (c + 1) * 512].rearrange("p (s q j) -> p s q j", s=PACK, j=PACK),
-                    in_=a_raw[:, c, :].rearrange("p (j q s) -> p s q j", j=PACK, s=PACK),
-                )
-            quantize(aq)
+        def interleave(copy, operand, raw):
+            copy(
+                out=operand[0][:].rearrange("p (c i j) -> p c j i", i=PAIR, j=PACK),
+                in_=raw.rearrange("p j (c i) -> p c j i", i=PAIR),
+            )
+
+        def interleave_a(copy, c):
+            copy(
+                out=a_grouped[:, c * R * PACK : (c + 1) * R * PACK].rearrange(
+                    "p (u i q j) -> p u q j i", u=PACK // PAIR, i=PAIR, j=PACK
+                ),
+                in_=a_raw[:, c, :].rearrange("p (j q u i) -> p u q j i", j=PACK, u=PACK // PAIR, i=PAIR),
+            )
+
+        def quantize(operand):
+            grouped, codes, scales = operand
+            nc.vector.quantize_mx(out=codes[:].bitcast(FP8X4), scales=scales[:], in_=grouped[:])
 
         def repeat_a():
-            grouped, codes, scales = aq
+            scale_words = ROWS // 4
             nc.vector.tensor_copy(
-                out=a_codes[:],
-                in_=codes[:].rearrange("p (e q) -> p e q", q=ROWS).unsqueeze(2).to_broadcast([P, 8, BLOCKS, ROWS]),
+                out=a_codes_x4[:],
+                in_=a_codes[:]
+                .rearrange("p (e q) -> p e q", q=ROWS)
+                .unsqueeze(2)
+                .to_broadcast([P, a_operands, BLOCKS, ROWS]),
             )
             nc.vector.tensor_copy(
-                out=a_scales[:].bitcast(I32).rearrange("p (e g q) -> p e g q", e=8, g=BLOCKS),
-                in_=scales[:].bitcast(I32).rearrange("p (e q) -> p e q", e=8).unsqueeze(2).to_broadcast([P, 8, BLOCKS, 8]),
+                out=a_scales_x4[:].bitcast(I32).rearrange("p (e g q) -> p e g q", e=a_operands, g=BLOCKS),
+                in_=a_scales[:]
+                .bitcast(I32)
+                .rearrange("p (e q) -> p e q", e=a_operands)
+                .unsqueeze(2)
+                .to_broadcast([P, a_operands, BLOCKS, scale_words]),
             )
 
-        def copy_blk(eng, ops, raws, c, b):
-            raw = raws[c, b // 2]
-            interleave(eng, ops[c, b][0][:], raw[:, :, (b % 2) * BLK : (b % 2 + 1) * BLK])
+        def a_operand(c, s):
+            e = c * PACK + s
+            return a_codes_x4[:, e].rearrange("p g q -> p (g q)"), a_scales_x4[:, e * BLK : (e + 1) * BLK]
 
-        def z_mm(b):
+        def matmul(psum, stationary, moving, start, stop):
+            nc.tensor.matmul_mx(
+                out=psum,
+                lhsT=stationary[0].bitcast(FP8X4),
+                lhsT_scale=stationary[1],
+                rhs=moving[0].bitcast(FP8X4),
+                rhs_scale=moving[1],
+                start=start,
+                stop=stop,
+            )
+
+        def planes(operand, partitions=slice(0, P)):
+            return operand[1][partitions, :], operand[2][partitions, :]
+
+        def block(i):
+            return slice(i * BLK, (i + 1) * BLK)
+
+        def warm_up(bank, count):
+            for i in range(count):
+                matmul(whole_bank[bank][:, block(0)], a_operand(0, 0), a_operand(0, 1), True, True)
+
+        def z_matmuls(b):
             for s in range(PACK):
                 for c in range(PASSES):
-                    e = c * PACK + s
-                    nc.tensor.matmul_mx(
-                        out=whole[b][:, s * BLK : (s + 1) * BLK],
-                        lhsT=a_codes[:, e].rearrange("p g q -> p (g q)").bitcast(FP8X4),
-                        lhsT_scale=a_scales[:, e * BLK : (e + 1) * BLK],
-                        rhs=xq[c, b][1][:].bitcast(FP8X4),
-                        rhs_scale=xq[c, b][2][:],
-                        start=(c == 0),
-                        stop=(c == PASSES - 1),
-                    )
+                    matmul(whole_bank[b][:, block(s)], a_operand(c, s), planes(x_mx[c, b]), c == 0, c == PASSES - 1)
 
         def z_out(b):
             nc.scalar.copy(
-                out=zq[b][0][:].rearrange("p (n s) -> p n s", s=PACK),
-                in_=whole[b][:].rearrange("p (s n) -> p n s", s=PACK),
+                out=z_mx[b][0][:].rearrange("p (n s) -> p n s", s=PACK),
+                in_=whole_bank[b][:].rearrange("p (s n) -> p n s", s=PACK),
             )
 
-        def lora_mm(b):
+        def lora_matmuls(b):
             for g in range(BLOCKS):
-                rows = slice(g * ROWS, (g + 1) * ROWS)
-                nc.tensor.matmul_mx(
-                    out=rowbank[g][:, b * BLK : (b + 1) * BLK],
-                    lhsT=bq[1][rows, :].bitcast(FP8X4),
-                    lhsT_scale=bq[2][rows, :],
-                    rhs=zq[b][1][rows, :].bitcast(FP8X4),
-                    rhs_scale=zq[b][2][rows, :],
-                    start=True,
-                    stop=True,
-                )
+                tile_rows = slice(g * ROWS, (g + 1) * ROWS)
+                matmul(row_bank[g][:, block(b)], planes(bb_mx, tile_rows), planes(z_mx[b], tile_rows), True, True)
 
         def lora_out(m):
-            nc.scalar.copy(out=lora[m][:], in_=rowbank[m][:])
+            nc.scalar.copy(out=lora[m][:], in_=row_bank[m][:])
 
-        def main_mm(m):
-            for b in range(BLOCKS):
+        def main_matmuls(m, bank, n_blocks):
+            for b in n_blocks:
                 for c in range(PASSES):
-                    nc.tensor.matmul_mx(
-                        out=whole[m][:, b * BLK : (b + 1) * BLK],
-                        lhsT=wq[c, m][1][:].bitcast(FP8X4),
-                        lhsT_scale=wq[c, m][2][:],
-                        rhs=xq[c, b][1][:].bitcast(FP8X4),
-                        rhs_scale=xq[c, b][2][:],
-                        start=(c == 0),
-                        stop=(c == PASSES - 1),
-                    )
+                    matmul(whole_bank[bank][:, block(b)], planes(w_mx[c, m]), planes(x_mx[c, b]), c == 0, c == PASSES - 1)
 
-        def add(m):
-            nc.vector.tensor_tensor(out=ysum[m][:], in0=whole[m][:], in1=lora[m][:], op=ALU.add)
+        def add(m, bank, cols):
+            nc.vector.tensor_tensor(out=y[m][:, cols], in0=whole_bank[bank][:, cols], in1=lora[m][:, cols], op=ALU.add)
 
-        def relu2(m):
+        def relu2_vector(m, cols):
             nc.vector.scalar_tensor_tensor(
-                out=res[m][:], in0=ysum[m][:], scalar=0.0, in1=ysum[m][:], op0=ALU.max, op1=ALU.mult
+                out=result[m][:, cols], in0=y[m][:, cols], scalar=0.0, in1=y[m][:, cols], op0=ALU.max, op1=ALU.mult
             )
-            nc.sync.dma_start(out=out[m * BLK : (m + 1) * BLK, :], in_=res[m][:])
 
-        def piece(ops, raws, c, h):
-            copy_blk("s", ops, raws, c, 2 * h)
-            copy_blk("v", ops, raws, c, 2 * h + 1)
-            quantize(ops[c, 2 * h])
-            quantize(ops[c, 2 * h + 1])
+        def relu2_left_scalar(m):
+            nc.scalar.activation(out=relu_left[m][:], in_=y[m][:, LEFT], func=ACT.Relu)
+            nc.scalar.activation(out=result[m][:, LEFT], in_=relu_left[m][:], func=ACT.Square)
 
-        prep_a()
-        copy_blk("s", xq, x_raw, 0, 0)
-        copy_blk("v", xq, x_raw, 0, 1)
+        def store(m):
+            nc.sync.dma_start(out=out[block(m), :], in_=result[m][:])
+
+        nc.vector.memset(a_scales[:].bitcast(I32), 0)
+        interleave_a(on_vector, 0)
+        interleave_a(on_scalar, 1)
+        quantize(a_mx)
         repeat_a()
-        quantize(xq[0, 0])
-        quantize(xq[0, 1])
-        piece(xq, x_raw, 1, 0)
-        z_mm(0)
-        z_mm(1)
-        piece(xq, x_raw, 0, 1)
-        z_out(0)
-        piece(xq, x_raw, 1, 1)
-        z_out(1)
-        z_mm(2)
-        z_mm(3)
-        interleave("v", bq[0][:], bb_raw[:])
-        quantize(zq[0])
-        quantize(bq)
-        quantize(zq[1])
-        z_out(2)
-        z_out(3)
-        lora_mm(0)
-        lora_mm(1)
-        copy_blk("v", wq, w_raw, 0, 0)
-        copy_blk("v", wq, w_raw, 0, 1)
-        quantize(zq[2])
-        quantize(wq[0, 0])
-        quantize(zq[3])
-        quantize(wq[0, 1])
-        lora_mm(2)
-        lora_mm(3)
-        piece(wq, w_raw, 1, 0)
-        main_mm(0)
-        main_mm(1)
-        lora_out(0)
-        lora_out(1)
-        piece(wq, w_raw, 0, 1)
-        add(0)
-        add(1)
+        warm_up(3, WARM_BEFORE_Z)
+
+        for b in range(BLOCKS):
+            interleave(on_vector if b % 2 else on_scalar, x_mx[0, b], x_raw[0, b])
+        for b in (1, 0, 3, 2):
+            quantize(x_mx[0, b])
+
+        for first in (0, 2):
+            interleave(on_vector, x_mx[1, first], x_raw[1, first])
+            interleave(on_scalar, x_mx[1, first + 1], x_raw[1, first + 1])
+            for b in (first, first + 1):
+                quantize(x_mx[1, b])
+                z_matmuls(b)
+
+        for b in range(BLOCKS):
+            z_out(b)
+        interleave(on_vector, bb_mx, bb_raw[:])
+        quantize(z_mx[0])
+        quantize(bb_mx)
+        quantize(z_mx[1])
+        lora_matmuls(0)
+        lora_matmuls(1)
+        warm_up(0, WARM_BEFORE_LAST_LORA)
+        for m, b in ((0, 2), (1, 3)):
+            interleave(on_vector, w_mx[0, m], w_raw[0, m])
+            quantize(z_mx[b])
+            lora_matmuls(b)
+
+        for m in (0, 1):
+            quantize(w_mx[0, m])
+            lora_out(m)
+        for m in (0, 1):
+            interleave(on_vector, w_mx[1, m], w_raw[1, m])
+        for m in (0, 1):
+            quantize(w_mx[1, m])
+            main_matmuls(m, m, range(BLOCKS))
+
+        interleave(on_scalar, w_mx[0, 2], w_raw[0, 2])
+        interleave(on_vector, w_mx[0, 3], w_raw[0, 3])
         lora_out(2)
-        relu2(0)
-        piece(wq, w_raw, 1, 1)
-        main_mm(2)
-        main_mm(3)
+        add(0, 0, ALL)
+        quantize(w_mx[0, 2])
+        quantize(w_mx[0, 3])
+        relu2_vector(0, ALL)
+        store(0)
+        interleave(on_scalar, w_mx[1, 2], w_raw[1, 2])
+        quantize(w_mx[1, 2])
+        main_matmuls(2, 2, range(BLOCKS))
+        add(1, 1, ALL)
+        interleave(on_scalar, w_mx[1, 3], w_raw[1, 3])
+        quantize(w_mx[1, 3])
+        main_matmuls(3, 0, (0, 1))
+        main_matmuls(3, 3, (2, 3))
         lora_out(3)
-        relu2(1)
-        add(2)
-        add(3)
-        relu2(2)
-        relu2(3)
+
+        relu2_left_scalar(1)
+        relu2_vector(1, RIGHT)
+        store(1)
+        add(2, 2, ALL)
+        relu2_left_scalar(2)
+        add(3, 0, LEFT)
+        relu2_vector(2, RIGHT)
+        store(2)
+        add(3, 3, RIGHT)
+        relu2_left_scalar(3)
+        relu2_vector(3, RIGHT)
+        store(3)

from contextlib import ExitStack

import concourse.mybir as mybir

K, R, M, N = 1024, 128, 512, 512
FLOPS = 2 * N * (K * M + K * R + R * M)

F32 = mybir.dt.float32
BF16 = mybir.dt.bfloat16
I32 = mybir.dt.int32
U8 = mybir.dt.uint8
FP8X4 = mybir.dt.float8_e4m3fn_x4
ALU = mybir.AluOpType
ACT = mybir.ActivationFunctionType

P = 128
PACK = 4
K_PASS = P * PACK
PASSES = K // K_PASS
BLK = 128
BLOCKS = N // BLK
ROWS = R // PACK
PAIR = 2
ALL = slice(0, N)
LEFT, RIGHT = slice(0, N // 2), slice(N // 2, N)
WARM_BEFORE_Z = 14
WARM_BEFORE_LAST_LORA = 8

assert M == N and BLOCKS * ROWS == P


def tile_rows_lora_relu2_kernel(tc, x, w, a, bb, out):
    nc = tc.nc
    on_vector, on_scalar = nc.vector.tensor_copy, nc.scalar.copy
    with ExitStack() as ctx:
        sb = ctx.enter_context(tc.tile_pool(name="sb", bufs=1))
        ps = ctx.enter_context(tc.psum_pool(name="ps", bufs=1))
        ctx.enter_context(tc.manual_schedule())

        whole_bank = [ps.tile([P, N], F32, name="whole%d" % i) for i in range(BLOCKS)]
        row_bank = [ps.tile([P, N], F32, name="row%d" % g) for g in range(BLOCKS)]

        def mx_operand(name, columns):
            grouped = sb.tile([P, columns * PACK], BF16, name=name + "_grouped", align_bytes=64)
            codes = sb.tile([P, columns], I32, name=name + "_codes", align_bytes=64)
            scales = sb.tile([P, columns], U8, name=name + "_scales", align_bytes=64)
            return grouped, codes, scales

        def load(src, name, c, first, count):
            raw = sb.tile([P, PACK, count * BLK], F32, name="%s_raw%d%d" % (name, c, first))
            rows = src[c * K_PASS : (c + 1) * K_PASS, first * BLK : (first + count) * BLK]
            nc.sync.dma_start(out=raw[:], in_=rows.rearrange("(p j) n -> p j n", j=PACK))
            return {(c, first + i): raw[:, :, i * BLK : (i + 1) * BLK] for i in range(count)}

        a_raw = sb.tile([P, PASSES, PACK * R], F32, name="a_raw")
        nc.sync.dma_start(out=a_raw[:], in_=a.rearrange("(c p j) r -> p c (j r)", c=PASSES, j=PACK))
        x_raw = {**load(x, "x", 0, 0, 4), **load(x, "x", 1, 0, 2), **load(x, "x", 1, 2, 2)}
        bb_raw = sb.tile([P, PACK, BLK], F32, name="bb_raw")
        for g in range(BLOCKS):
            nc.sync.dma_start(
                out=bb_raw[g * ROWS : (g + 1) * ROWS],
                in_=bb[:, g * BLK : (g + 1) * BLK].rearrange("(p j) m -> p j m", j=PACK),
            )
        w_raw = {**load(w, "w", 0, 0, 2), **load(w, "w", 1, 0, 2)}
        w_raw = {**w_raw, **load(w, "w", 0, 2, 2), **load(w, "w", 1, 2, 1), **load(w, "w", 1, 3, 1)}

        x_mx = {key: mx_operand("x%d%d" % key, BLK) for key in sorted(x_raw)}
        w_mx = {key: mx_operand("w%d%d" % key, BLK) for key in sorted(w_raw)}
        z_mx = [mx_operand("z%d" % b, BLK) for b in range(BLOCKS)]
        bb_mx = mx_operand("bb", BLK)
        a_grouped, a_codes, a_scales = a_mx = mx_operand("a", PASSES * R)
        a_operands = PASSES * PACK
        a_codes_x4 = sb.tile([P, a_operands, BLOCKS, ROWS], I32, name="a_codes_x4", align_bytes=64)
        a_scales_x4 = sb.tile([P, a_operands * BLK], U8, name="a_scales_x4", align_bytes=64)
        lora = [sb.tile([P, N], F32, name="lora%d" % m) for m in range(BLOCKS)]
        y = [sb.tile([P, N], F32, name="y%d" % m) for m in range(BLOCKS)]
        result = [sb.tile([P, N], F32, name="result%d" % m) for m in range(BLOCKS)]
        relu_left = {m: sb.tile([P, N // 2], F32, name="relu%d" % m) for m in range(1, BLOCKS)}

        def interleave(copy, operand, raw):
            copy(
                out=operand[0][:].rearrange("p (c i j) -> p c j i", i=PAIR, j=PACK),
                in_=raw.rearrange("p j (c i) -> p c j i", i=PAIR),
            )

        def interleave_a(copy, c):
            copy(
                out=a_grouped[:, c * R * PACK : (c + 1) * R * PACK].rearrange(
                    "p (u i q j) -> p u q j i", u=PACK // PAIR, i=PAIR, j=PACK
                ),
                in_=a_raw[:, c, :].rearrange("p (j q u i) -> p u q j i", j=PACK, u=PACK // PAIR, i=PAIR),
            )

        def quantize(operand):
            grouped, codes, scales = operand
            nc.vector.quantize_mx(out=codes[:].bitcast(FP8X4), scales=scales[:], in_=grouped[:])

        def repeat_a():
            scale_words = ROWS // 4
            nc.vector.tensor_copy(
                out=a_codes_x4[:],
                in_=a_codes[:]
                .rearrange("p (e q) -> p e q", q=ROWS)
                .unsqueeze(2)
                .to_broadcast([P, a_operands, BLOCKS, ROWS]),
            )
            nc.vector.tensor_copy(
                out=a_scales_x4[:].bitcast(I32).rearrange("p (e g q) -> p e g q", e=a_operands, g=BLOCKS),
                in_=a_scales[:]
                .bitcast(I32)
                .rearrange("p (e q) -> p e q", e=a_operands)
                .unsqueeze(2)
                .to_broadcast([P, a_operands, BLOCKS, scale_words]),
            )

        def a_operand(c, s):
            e = c * PACK + s
            return a_codes_x4[:, e].rearrange("p g q -> p (g q)"), a_scales_x4[:, e * BLK : (e + 1) * BLK]

        def matmul(psum, stationary, moving, start, stop):
            nc.tensor.matmul_mx(
                out=psum,
                lhsT=stationary[0].bitcast(FP8X4),
                lhsT_scale=stationary[1],
                rhs=moving[0].bitcast(FP8X4),
                rhs_scale=moving[1],
                start=start,
                stop=stop,
            )

        def planes(operand, partitions=slice(0, P)):
            return operand[1][partitions, :], operand[2][partitions, :]

        def block(i):
            return slice(i * BLK, (i + 1) * BLK)

        def warm_up(bank, count):
            for i in range(count):
                matmul(whole_bank[bank][:, block(0)], a_operand(0, 0), a_operand(0, 1), True, True)

        def z_matmuls(b):
            for s in range(PACK):
                for c in range(PASSES):
                    matmul(whole_bank[b][:, block(s)], a_operand(c, s), planes(x_mx[c, b]), c == 0, c == PASSES - 1)

        def z_out(b):
            nc.scalar.copy(
                out=z_mx[b][0][:].rearrange("p (n s) -> p n s", s=PACK),
                in_=whole_bank[b][:].rearrange("p (s n) -> p n s", s=PACK),
            )

        def lora_matmuls(b):
            for g in range(BLOCKS):
                tile_rows = slice(g * ROWS, (g + 1) * ROWS)
                matmul(row_bank[g][:, block(b)], planes(bb_mx, tile_rows), planes(z_mx[b], tile_rows), True, True)

        def lora_out(m):
            nc.scalar.copy(out=lora[m][:], in_=row_bank[m][:])

        def main_matmuls(m, bank, n_blocks):
            for b in n_blocks:
                for c in range(PASSES):
                    matmul(whole_bank[bank][:, block(b)], planes(w_mx[c, m]), planes(x_mx[c, b]), c == 0, c == PASSES - 1)

        def add(m, bank, cols):
            nc.vector.tensor_tensor(out=y[m][:, cols], in0=whole_bank[bank][:, cols], in1=lora[m][:, cols], op=ALU.add)

        def relu2_vector(m, cols):
            nc.vector.scalar_tensor_tensor(
                out=result[m][:, cols], in0=y[m][:, cols], scalar=0.0, in1=y[m][:, cols], op0=ALU.max, op1=ALU.mult
            )

        def relu2_left_scalar(m):
            nc.scalar.activation(out=relu_left[m][:], in_=y[m][:, LEFT], func=ACT.Relu)
            nc.scalar.activation(out=result[m][:, LEFT], in_=relu_left[m][:], func=ACT.Square)

        def store(m):
            nc.sync.dma_start(out=out[block(m), :], in_=result[m][:])

        nc.vector.memset(a_scales[:].bitcast(I32), 0)
        interleave_a(on_vector, 0)
        interleave_a(on_scalar, 1)
        quantize(a_mx)
        repeat_a()
        warm_up(3, WARM_BEFORE_Z)

        for b in range(BLOCKS):
            interleave(on_vector if b % 2 else on_scalar, x_mx[0, b], x_raw[0, b])
        for b in (1, 0, 3, 2):
            quantize(x_mx[0, b])

        for first in (0, 2):
            interleave(on_vector, x_mx[1, first], x_raw[1, first])
            interleave(on_scalar, x_mx[1, first + 1], x_raw[1, first + 1])
            for b in (first, first + 1):
                quantize(x_mx[1, b])
                z_matmuls(b)

        for b in range(BLOCKS):
            z_out(b)
        interleave(on_vector, bb_mx, bb_raw[:])
        quantize(z_mx[0])
        quantize(bb_mx)
        quantize(z_mx[1])
        lora_matmuls(0)
        lora_matmuls(1)
        warm_up(0, WARM_BEFORE_LAST_LORA)
        for m, b in ((0, 2), (1, 3)):
            interleave(on_vector, w_mx[0, m], w_raw[0, m])
            quantize(z_mx[b])
            lora_matmuls(b)

        for m in (0, 1):
            quantize(w_mx[0, m])
            lora_out(m)
        for m in (0, 1):
            interleave(on_vector, w_mx[1, m], w_raw[1, m])
        for m in (0, 1):
            quantize(w_mx[1, m])
            main_matmuls(m, m, range(BLOCKS))

        interleave(on_scalar, w_mx[0, 2], w_raw[0, 2])
        interleave(on_vector, w_mx[0, 3], w_raw[0, 3])
        lora_out(2)
        add(0, 0, ALL)
        quantize(w_mx[0, 2])
        quantize(w_mx[0, 3])
        relu2_vector(0, ALL)
        store(0)
        interleave(on_scalar, w_mx[1, 2], w_raw[1, 2])
        quantize(w_mx[1, 2])
        main_matmuls(2, 2, range(BLOCKS))
        add(1, 1, ALL)
        interleave(on_scalar, w_mx[1, 3], w_raw[1, 3])
        quantize(w_mx[1, 3])
        main_matmuls(3, 0, (0, 1))
        main_matmuls(3, 3, (2, 3))
        lora_out(3)

        relu2_left_scalar(1)
        relu2_vector(1, RIGHT)
        store(1)
        add(2, 2, ALL)
        relu2_left_scalar(2)
        add(3, 0, LEFT)
        relu2_vector(2, RIGHT)
        store(2)
        add(3, 3, RIGHT)
        relu2_left_scalar(3)
        relu2_vector(3, RIGHT)
        store(3)
